import numpy as np
import ml_dtypes

BF16 = ml_dtypes.bfloat16


def bf(x):
    return np.asarray(x, np.float32).astype(BF16)


def f32(x):
    return np.asarray(x, np.float32)


def f64(x):
    return np.asarray(x).astype(np.float64)


def striped(idx):
    return np.tile(idx.reshape(-1, 16).T, (8, 1))


S, K, M, N, B, Q = 256, 128, 256, 128, 2, 64


def setup_inputs():
    return {"base": bf(np.random.standard_normal((B, M, S))), "x": bf(np.random.standard_normal((K, N))), "w": bf(np.random.standard_normal((K, M)) / np.sqrt(K)), "offs": striped(np.random.permutation(S)[:N])}


def reference(base, x, w, offs):
    idx = offs[:16].T.reshape(-1)
    z = f64(base).copy()
    for i in range(B):
        z[i][:, idx[i * Q : (i + 1) * Q]] = f64(w).T @ f64(x)[:, i * Q : (i + 1) * Q]
    return z

@@ -1,0 +1,62 @@
+import concourse.mybir as mybir
+from concourse.masks import make_identity
+
+BF16, F32, U16 = mybir.dt.bfloat16, mybir.dt.float32, mybir.dt.uint16
+
+P = 128
+SEQS = 2
+TOKENS = 256
+FEATURES = 256
+BLOCKS = FEATURES // P
+LIST = 128
+PIECE = LIST // SEQS
+PIECE_COLS = PIECE // 16
+
+FLOPS = 2 * P * FEATURES * LIST
+
+
+def tile_scatter_matmul_kernel(tc, base, x, w, offs, out):
+    nc = tc.nc
+    with (
+        tc.tile_pool(name="held", bufs=1) as held,
+        tc.psum_pool(name="windows", bufs=1) as windows,
+    ):
+        offsets = held.tile([P, LIST // 16], U16, name="offsets")
+        nc.sync.dma_start(offsets[:], offs)
+
+        ident = held.tile([P, P], BF16, name="ident")
+        make_identity(nc, ident[:])
+
+        base_sb = [held.tile([P, BLOCKS, TOKENS], BF16, name=f"base_sb{i}") for i in range(SEQS)]
+        nc.sync.dma_start(base_sb[0][:], base[0].rearrange("(a p) s -> p a s", p=P))
+        nc.scalar.dma_start(base_sb[1][:], base[1].rearrange("(a p) s -> p a s", p=P))
+        w_sb = held.tile([P, FEATURES], BF16, name="w_sb")
+        nc.scalar.dma_start(w_sb[:], w)
+        x_sb = held.tile([P, LIST], BF16, name="x_sb")
+        nc.sync.dma_start(x_sb[:], x)
+
+        pairs = [(i, a) for i in range(SEQS) for a in range(BLOCKS)]
+        window = {
+            (i, a): windows.tile([P, TOKENS], F32, name=f"window{i}{a}") for (i, a) in pairs
+        }
+
+        for i, a in pairs:
+            nc.tensor.matmul(window[i, a][:], ident[:], base_sb[i][:, a, :], start=True, stop=True)
+
+        for i, a in pairs:
+            nc.tensor.matmul(
+                window[i, a][:].indirect(offsets[:, i * PIECE_COLS : (i + 1) * PIECE_COLS]),
+                w_sb[:, a * P : (a + 1) * P],
+                x_sb[:, i * PIECE : (i + 1) * PIECE],
+                start=True,
+                stop=True,
+            )
+
+        for i, a in pairs:
+            z_sb = held.tile([P, TOKENS], F32, name=f"z_sb{i}{a}")
+            if a == 0:
+                nc.vector.tensor_copy(z_sb[:], window[i, a][:])
+                nc.sync.dma_start(out[i, a * P : (a + 1) * P, :], z_sb[:])
+            else:
+                nc.scalar.copy(z_sb[:], window[i, a][:])
+                nc.scalar.dma_start(out[i, a * P : (a + 1) * P, :], z_sb[:])

@@ -12,6 +12,9 @@ LIST = 128
 PIECE = LIST // SEQS
 PIECE_COLS = PIECE // 16
 
+BANK = 512
+WARM = 5
+
 FLOPS = 2 * P * FEATURES * LIST
 
 
@@ -23,6 +26,12 @@ def tile_scatter_matmul_kernel(tc, base, x, w, offs, out):
     ):
         offsets = held.tile([P, LIST // 16], U16, name="offsets")
         nc.sync.dma_start(offsets[:], offs)
+
+        zeros = held.tile([P, BANK], BF16, name="zeros")
+        nc.vector.memset(zeros[:], 0.0)
+        warm = windows.tile([P, BANK], F32, name="warm")
+        for n in range(WARM):
+            nc.tensor.matmul(warm[:], zeros[:, 0:P], zeros[:], start=True, stop=True)
 
         ident = held.tile([P, P], BF16, name="ident")
         make_identity(nc, ident[:])

@@ -12,9 +12,6 @@ LIST = 128
 PIECE = LIST // SEQS
 PIECE_COLS = PIECE // 16
 
-BANK = 512
-WARM = 5
-
 FLOPS = 2 * P * FEATURES * LIST
 
 
@@ -24,33 +21,29 @@ def tile_scatter_matmul_kernel(tc, base, x, w, offs, out):
         tc.tile_pool(name="held", bufs=1) as held,
         tc.psum_pool(name="windows", bufs=1) as windows,
     ):
-        offsets = held.tile([P, LIST // 16], U16, name="offsets")
-        nc.sync.dma_start(offsets[:], offs)
-
-        zeros = held.tile([P, BANK], BF16, name="zeros")
-        nc.vector.memset(zeros[:], 0.0)
-        warm = windows.tile([P, BANK], F32, name="warm")
-        for n in range(WARM):
-            nc.tensor.matmul(warm[:], zeros[:, 0:P], zeros[:], start=True, stop=True)
-
         ident = held.tile([P, P], BF16, name="ident")
         make_identity(nc, ident[:])
 
-        base_sb = [held.tile([P, BLOCKS, TOKENS], BF16, name=f"base_sb{i}") for i in range(SEQS)]
-        nc.sync.dma_start(base_sb[0][:], base[0].rearrange("(a p) s -> p a s", p=P))
-        nc.scalar.dma_start(base_sb[1][:], base[1].rearrange("(a p) s -> p a s", p=P))
+        pairs = [(i, a) for i in range(SEQS) for a in range(BLOCKS)]
+
+        queue = [nc.sync, nc.scalar]
+        base_sb = {(i, a): held.tile([P, TOKENS], BF16, name=f"base_sb{i}{a}") for (i, a) in pairs}
+        for i, a in pairs:
+            queue[a].dma_start(base_sb[i, a][:], base[i, a * P : (a + 1) * P, :])
+
+        offsets = held.tile([P, LIST // 16], U16, name="offsets")
+        nc.sync.dma_start(offsets[:], offs)
         w_sb = held.tile([P, FEATURES], BF16, name="w_sb")
         nc.scalar.dma_start(w_sb[:], w)
         x_sb = held.tile([P, LIST], BF16, name="x_sb")
         nc.sync.dma_start(x_sb[:], x)
 
-        pairs = [(i, a) for i in range(SEQS) for a in range(BLOCKS)]
         window = {
             (i, a): windows.tile([P, TOKENS], F32, name=f"window{i}{a}") for (i, a) in pairs
         }
 
         for i, a in pairs:
-            nc.tensor.matmul(window[i, a][:], ident[:], base_sb[i][:, a, :], start=True, stop=True)
+            nc.tensor.matmul(window[i, a][:], ident[:], base_sb[i, a][:], start=True, stop=True)
 
         for i, a in pairs:
             nc.tensor.matmul(

@@ -31,12 +31,12 @@ def tile_scatter_matmul_kernel(tc, base, x, w, offs, out):
         for i, a in pairs:
             queue[a].dma_start(base_sb[i, a][:], base[i, a * P : (a + 1) * P, :])
 
-        offsets = held.tile([P, LIST // 16], U16, name="offsets")
-        nc.sync.dma_start(offsets[:], offs)
-        w_sb = held.tile([P, FEATURES], BF16, name="w_sb")
-        nc.scalar.dma_start(w_sb[:], w)
         x_sb = held.tile([P, LIST], BF16, name="x_sb")
         nc.sync.dma_start(x_sb[:], x)
+        w_sb = held.tile([P, FEATURES], BF16, name="w_sb")
+        nc.scalar.dma_start(w_sb[:], w)
+        offsets = held.tile([P, LIST // 16], U16, name="offsets")
+        nc.sync.dma_start(offsets[:], offs)
 
         window = {
             (i, a): windows.tile([P, TOKENS], F32, name=f"window{i}{a}") for (i, a) in pairs

@@ -12,6 +12,9 @@ LIST = 128
 PIECE = LIST // SEQS
 PIECE_COLS = PIECE // 16
 
+WARM_COLS = 256
+WARM_MATMULS = 4
+
 FLOPS = 2 * P * FEATURES * LIST
 
 
@@ -23,6 +26,12 @@ def tile_scatter_matmul_kernel(tc, base, x, w, offs, out):
     ):
         ident = held.tile([P, P], BF16, name="ident")
         make_identity(nc, ident[:])
+
+        zeros = held.tile([P, WARM_COLS], BF16, name="zeros")
+        nc.vector.memset(zeros[:], 0.0)
+        unread = windows.tile([P, WARM_COLS], F32, name="unread")
+        for k in range(WARM_MATMULS):
+            nc.tensor.matmul(unread[:], zeros[:, 0:P], zeros[:], start=True, stop=True)
 
         pairs = [(i, a) for i in range(SEQS) for a in range(BLOCKS)]
 

@@ -7,7 +7,7 @@ P = 128
 SEQS = 2
 TOKENS = 256
 FEATURES = 256
-BLOCKS = FEATURES // P
+PAIR = FEATURES // P
 LIST = 128
 PIECE = LIST // SEQS
 PIECE_COLS = PIECE // 16
@@ -33,41 +33,48 @@ def tile_scatter_matmul_kernel(tc, base, x, w, offs, out):
         for k in range(WARM_MATMULS):
             nc.tensor.matmul(unread[:], zeros[:, 0:P], zeros[:], start=True, stop=True)
 
-        pairs = [(i, a) for i in range(SEQS) for a in range(BLOCKS)]
-
-        queue = [nc.sync, nc.scalar]
-        base_sb = {(i, a): held.tile([P, TOKENS], BF16, name=f"base_sb{i}{a}") for (i, a) in pairs}
-        for i, a in pairs:
-            queue[a].dma_start(base_sb[i, a][:], base[i, a * P : (a + 1) * P, :])
-
+        base_sb = {i: held.tile([P, PAIR * TOKENS], BF16, name=f"base_sb{i}") for i in range(SEQS)}
+        for i in range(SEQS):
+            nc.sync.dma_start(base_sb[i][:], base[i].rearrange("(p e) t -> p (e t)", e=PAIR))
+        w_sb = held.tile([P, FEATURES], BF16, name="w_sb")
+        nc.sync.dma_start(w_sb[:], w)
         x_sb = held.tile([P, LIST], BF16, name="x_sb")
         nc.sync.dma_start(x_sb[:], x)
-        w_sb = held.tile([P, FEATURES], BF16, name="w_sb")
-        nc.scalar.dma_start(w_sb[:], w)
         offsets = held.tile([P, LIST // 16], U16, name="offsets")
         nc.sync.dma_start(offsets[:], offs)
 
+        w_sorted = held.tile([P, PAIR, P], BF16, name="w_sorted")
+        nc.vector.tensor_copy(w_sorted[:], w_sb[:].rearrange("k (m e) -> k e m", e=PAIR))
+
+        pairs = [(i, e) for i in range(SEQS) for e in range(PAIR)]
         window = {
-            (i, a): windows.tile([P, TOKENS], F32, name=f"window{i}{a}") for (i, a) in pairs
+            (i, e): windows.tile([P, TOKENS], F32, name=f"window{i}{e}") for (i, e) in pairs
         }
 
-        for i, a in pairs:
-            nc.tensor.matmul(window[i, a][:], ident[:], base_sb[i, a][:], start=True, stop=True)
-
-        for i, a in pairs:
+        for i, e in pairs:
             nc.tensor.matmul(
-                window[i, a][:].indirect(offsets[:, i * PIECE_COLS : (i + 1) * PIECE_COLS]),
-                w_sb[:, a * P : (a + 1) * P],
+                window[i, e][:],
+                ident[:],
+                base_sb[i][:, e * TOKENS : (e + 1) * TOKENS],
+                start=True,
+                stop=True,
+            )
+
+        for i, e in pairs:
+            nc.tensor.matmul(
+                window[i, e][:].indirect(offsets[:, i * PIECE_COLS : (i + 1) * PIECE_COLS]),
+                w_sorted[:, e, :],
                 x_sb[:, i * PIECE : (i + 1) * PIECE],
                 start=True,
                 stop=True,
             )
 
-        for i, a in pairs:
-            z_sb = held.tile([P, TOKENS], F32, name=f"z_sb{i}{a}")
-            if a == 0:
-                nc.vector.tensor_copy(z_sb[:], window[i, a][:])
-                nc.sync.dma_start(out[i, a * P : (a + 1) * P, :], z_sb[:])
+        for i, e in pairs:
+            out_rows = out[i].rearrange("(p e) t -> p e t", e=PAIR)[:, e, :]
+            z_sb = held.tile([P, TOKENS], F32, name=f"z_sb{i}{e}")
+            if e == 0:
+                nc.vector.tensor_copy(z_sb[:], window[i, e][:])
+                nc.sync.dma_start(out_rows, z_sb[:])
             else:
-                nc.scalar.copy(z_sb[:], window[i, a][:])
-                nc.scalar.dma_start(out[i, a * P : (a + 1) * P, :], z_sb[:])
+                nc.scalar.copy(z_sb[:], window[i, e][:])
+                nc.scalar.dma_start(out_rows, z_sb[:])

@@ -69,12 +69,9 @@ def tile_scatter_matmul_kernel(tc, base, x, w, offs, out):
                 stop=True,
             )
 
-        for i, e in pairs:
-            out_rows = out[i].rearrange("(p e) t -> p e t", e=PAIR)[:, e, :]
-            z_sb = held.tile([P, TOKENS], F32, name=f"z_sb{i}{e}")
-            if e == 0:
-                nc.vector.tensor_copy(z_sb[:], window[i, e][:])
-                nc.sync.dma_start(out_rows, z_sb[:])
-            else:
-                nc.scalar.copy(z_sb[:], window[i, e][:])
-                nc.scalar.dma_start(out_rows, z_sb[:])
+        queue = [nc.sync, nc.scalar]
+        for i in range(SEQS):
+            z_sb = held.tile([P, PAIR * TOKENS], F32, name=f"z_sb{i}")
+            nc.vector.tensor_copy(z_sb[:, 0:TOKENS], window[i, 0][:])
+            nc.scalar.copy(z_sb[:, TOKENS : PAIR * TOKENS], window[i, 1][:])
+            queue[i].dma_start(out[i].rearrange("(p e) t -> p (e t)", e=PAIR), z_sb[:])

@@ -34,17 +34,19 @@ def tile_scatter_matmul_kernel(tc, base, x, w, offs, out):
             nc.tensor.matmul(unread[:], zeros[:, 0:P], zeros[:], start=True, stop=True)
 
         base_sb = {i: held.tile([P, PAIR * TOKENS], BF16, name=f"base_sb{i}") for i in range(SEQS)}
-        for i in range(SEQS):
-            nc.sync.dma_start(base_sb[i][:], base[i].rearrange("(p e) t -> p (e t)", e=PAIR))
         w_sb = held.tile([P, FEATURES], BF16, name="w_sb")
-        nc.sync.dma_start(w_sb[:], w)
         x_sb = held.tile([P, LIST], BF16, name="x_sb")
-        nc.sync.dma_start(x_sb[:], x)
         offsets = held.tile([P, LIST // 16], U16, name="offsets")
+        nc.sync.dma_start(base_sb[0][:], base[0].rearrange("(p e) t -> p (e t)", e=PAIR))
+        nc.sync.dma_start(w_sb[:], w)
+        nc.sync.dma_start(base_sb[1][:], base[1].rearrange("(p e) t -> p (e t)", e=PAIR))
+        nc.sync.dma_start(x_sb[:], x)
         nc.sync.dma_start(offsets[:], offs)
 
-        w_sorted = held.tile([P, PAIR, P], BF16, name="w_sorted")
-        nc.vector.tensor_copy(w_sorted[:], w_sb[:].rearrange("k (m e) -> k e m", e=PAIR))
+        w_columns = w_sb[:].rearrange("k (m e) -> k e m", e=PAIR)
+        w_block = {e: held.tile([P, P], BF16, name=f"w_block{e}") for e in range(PAIR)}
+        for e in range(PAIR):
+            nc.vector.tensor_copy(w_block[e][:], w_columns[:, e, :])
 
         pairs = [(i, e) for i in range(SEQS) for e in range(PAIR)]
         window = {
@@ -63,7 +65,7 @@ def tile_scatter_matmul_kernel(tc, base, x, w, offs, out):
         for i, e in pairs:
             nc.tensor.matmul(
                 window[i, e][:].indirect(offsets[:, i * PIECE_COLS : (i + 1) * PIECE_COLS]),
-                w_sorted[:, e, :],
+                w_block[e][:],
                 x_sb[:, i * PIECE : (i + 1) * PIECE],
                 start=True,
                 stop=True,

@@ -15,6 +15,8 @@ PIECE_COLS = PIECE // 16
 WARM_COLS = 256
 WARM_MATMULS = 4
 
+DMA_ALIGN = 256
+
 FLOPS = 2 * P * FEATURES * LIST
 
 
@@ -33,9 +35,12 @@ def tile_scatter_matmul_kernel(tc, base, x, w, offs, out):
         for k in range(WARM_MATMULS):
             nc.tensor.matmul(unread[:], zeros[:, 0:P], zeros[:], start=True, stop=True)
 
-        base_sb = {i: held.tile([P, PAIR * TOKENS], BF16, name=f"base_sb{i}") for i in range(SEQS)}
-        w_sb = held.tile([P, FEATURES], BF16, name="w_sb")
-        x_sb = held.tile([P, LIST], BF16, name="x_sb")
+        base_sb = {
+            i: held.tile([P, PAIR * TOKENS], BF16, name=f"base_sb{i}", align_bytes=DMA_ALIGN)
+            for i in range(SEQS)
+        }
+        w_sb = held.tile([P, FEATURES], BF16, name="w_sb", align_bytes=DMA_ALIGN)
+        x_sb = held.tile([P, LIST], BF16, name="x_sb", align_bytes=DMA_ALIGN)
         offsets = held.tile([P, LIST // 16], U16, name="offsets")
         nc.sync.dma_start(base_sb[0][:], base[0].rearrange("(p e) t -> p (e t)", e=PAIR))
         nc.sync.dma_start(w_sb[:], w)
@@ -73,7 +78,7 @@ def tile_scatter_matmul_kernel(tc, base, x, w, offs, out):
 
         queue = [nc.sync, nc.scalar]
         for i in range(SEQS):
-            z_sb = held.tile([P, PAIR * TOKENS], F32, name=f"z_sb{i}")
+            z_sb = held.tile([P, PAIR * TOKENS], F32, name=f"z_sb{i}", align_bytes=DMA_ALIGN)
             nc.vector.tensor_copy(z_sb[:, 0:TOKENS], window[i, 0][:])
             nc.scalar.copy(z_sb[:, TOKENS : PAIR * TOKENS], window[i, 1][:])
             queue[i].dma_start(out[i].rearrange("(p e) t -> p (e t)", e=PAIR), z_sb[:])

@@ -12,8 +12,9 @@ LIST = 128
 PIECE = LIST // SEQS
 PIECE_COLS = PIECE // 16
 
+WARM_TILE = 32
 WARM_COLS = 256
-WARM_MATMULS = 4
+WARM_MATMULS = 5
 
 DMA_ALIGN = 256
 
@@ -29,11 +30,13 @@ def tile_scatter_matmul_kernel(tc, base, x, w, offs, out):
         ident = held.tile([P, P], BF16, name="ident")
         make_identity(nc, ident[:])
 
-        zeros = held.tile([P, WARM_COLS], BF16, name="zeros")
+        zeros = held.tile([P, WARM_TILE], BF16, name="zeros")
         nc.vector.memset(zeros[:], 0.0)
+        zero_weights = zeros[:, 0:1].to_broadcast([P, P])
+        zeros_repeated = zeros[:].unsqueeze(1).to_broadcast([P, WARM_COLS // WARM_TILE, WARM_TILE])
         unread = windows.tile([P, WARM_COLS], F32, name="unread")
         for k in range(WARM_MATMULS):
-            nc.tensor.matmul(unread[:], zeros[:, 0:P], zeros[:], start=True, stop=True)
+            nc.tensor.matmul(unread[:], zero_weights, zeros_repeated, start=True, stop=True)
 
         base_sb = {
             i: held.tile([P, PAIR * TOKENS], BF16, name=f"base_sb{i}", align_bytes=DMA_ALIGN)

import concourse.mybir as mybir
from concourse.masks import make_identity

BF16, F32, U16 = mybir.dt.bfloat16, mybir.dt.float32, mybir.dt.uint16

P = 128
SEQS = 2
TOKENS = 256
FEATURES = 256
PAIR = FEATURES // P
LIST = 128
PIECE = LIST // SEQS
PIECE_COLS = PIECE // 16

WARM_TILE = 32
WARM_COLS = 256
WARM_MATMULS = 5

DMA_ALIGN = 256

FLOPS = 2 * P * FEATURES * LIST


def tile_scatter_matmul_kernel(tc, base, x, w, offs, out):
    nc = tc.nc
    with (
        tc.tile_pool(name="held", bufs=1) as held,
        tc.psum_pool(name="windows", bufs=1) as windows,
    ):
        ident = held.tile([P, P], BF16, name="ident")
        make_identity(nc, ident[:])

        zeros = held.tile([P, WARM_TILE], BF16, name="zeros")
        nc.vector.memset(zeros[:], 0.0)
        zero_weights = zeros[:, 0:1].to_broadcast([P, P])
        zeros_repeated = zeros[:].unsqueeze(1).to_broadcast([P, WARM_COLS // WARM_TILE, WARM_TILE])
        unread = windows.tile([P, WARM_COLS], F32, name="unread")
        for k in range(WARM_MATMULS):
            nc.tensor.matmul(unread[:], zero_weights, zeros_repeated, start=True, stop=True)

        base_sb = {
            i: held.tile([P, PAIR * TOKENS], BF16, name=f"base_sb{i}", align_bytes=DMA_ALIGN)
            for i in range(SEQS)
        }
        w_sb = held.tile([P, FEATURES], BF16, name="w_sb", align_bytes=DMA_ALIGN)
        x_sb = held.tile([P, LIST], BF16, name="x_sb", align_bytes=DMA_ALIGN)
        offsets = held.tile([P, LIST // 16], U16, name="offsets")
        nc.sync.dma_start(base_sb[0][:], base[0].rearrange("(p e) t -> p (e t)", e=PAIR))
        nc.sync.dma_start(w_sb[:], w)
        nc.sync.dma_start(base_sb[1][:], base[1].rearrange("(p e) t -> p (e t)", e=PAIR))
        nc.sync.dma_start(x_sb[:], x)
        nc.sync.dma_start(offsets[:], offs)

        w_columns = w_sb[:].rearrange("k (m e) -> k e m", e=PAIR)
        w_block = {e: held.tile([P, P], BF16, name=f"w_block{e}") for e in range(PAIR)}
        for e in range(PAIR):
            nc.vector.tensor_copy(w_block[e][:], w_columns[:, e, :])

        pairs = [(i, e) for i in range(SEQS) for e in range(PAIR)]
        window = {
            (i, e): windows.tile([P, TOKENS], F32, name=f"window{i}{e}") for (i, e) in pairs
        }

        for i, e in pairs:
            nc.tensor.matmul(
                window[i, e][:],
                ident[:],
                base_sb[i][:, e * TOKENS : (e + 1) * TOKENS],
                start=True,
                stop=True,
            )

        for i, e in pairs:
            nc.tensor.matmul(
                window[i, e][:].indirect(offsets[:, i * PIECE_COLS : (i + 1) * PIECE_COLS]),
                w_block[e][:],
                x_sb[:, i * PIECE : (i + 1) * PIECE],
                start=True,
                stop=True,
            )

        queue = [nc.sync, nc.scalar]
        for i in range(SEQS):
            z_sb = held.tile([P, PAIR * TOKENS], F32, name=f"z_sb{i}", align_bytes=DMA_ALIGN)
            nc.vector.tensor_copy(z_sb[:, 0:TOKENS], window[i, 0][:])
            nc.scalar.copy(z_sb[:, TOKENS : PAIR * TOKENS], window[i, 1][:])
            queue[i].dma_start(out[i].rearrange("(p e) t -> p (e t)", e=PAIR), z_sb[:])
